import numpy as np, ml_dtypes
CORES = [25,29,65,69,153,157,193,197]
N = 8
import mx_ref
BF = ml_dtypes.bfloat16
def entries(a):
    return np.ascontiguousarray(a.T).reshape(-1)
def table(e):
    return np.ascontiguousarray(np.reshape(e, (-1, 16)).T).astype(np.int32)
def cols(t, e):
    v = np.concatenate([t.reshape(128, -1, 4), np.zeros((128, 1, 4), BF)], axis=1)
    return np.ascontiguousarray(v[:, e]).reshape(128, -1)
def f(rng, *shape):
    return mx_ref.flush((rng.standard_normal(shape, dtype=np.float32) * np.exp2(rng.integers(-2, 3, shape[:-1] + (1,)))).astype(BF))
def wide(rng, *shape, cols=0):
    v = rng.standard_normal(shape, dtype=np.float32) * np.exp2(rng.integers(-12, 13, shape)).astype(np.float32)
    if cols: v *= np.repeat(np.exp2(rng.integers(-cols, cols + 1, shape[:-2] + (1, shape[-1] // 4))) * (rng.random(shape[:-2] + (1, shape[-1] // 4)) > 0.0625), 4, axis=-1).astype(np.float32)
    return mx_ref.flush(v.astype(BF))
T, KP, TOT, QT = 256, 160, 1024, 8
CAPP, DR, CW = KP // N, T // 16, TOT // N
def counts(rng, lo, hi):
    L, U = [TOT], [TOT]
    for q in range(N)[::-1]:
        L.insert(0, max(q * CW - N * DR, L[0] - hi[q]))
        U.insert(0, min((q - 1) * CW + N * (DR + CAPP + 1), U[0] - lo[q]))
    n, s = [], 0
    for q in range(N):
        n.append(int(rng.integers(max(lo[q], L[q + 1] - s), min(hi[q], U[q + 1] - s) + 1))); s += n[-1]
    return n
def slots(k):
    s, p, g = np.full((N, N, CAPP), -1), np.zeros((N, CW), int), 0
    for q in range(N):
        used = [0] * N
        for c in k[q]:
            r = g % N
            s[q, r, used[r]] = c; p[r, g // N] = q * CAPP + used[r]
            used[r] += 1; g += 1
    return np.stack([table(a) for a in s]), np.stack([table(a) for a in p])
def lists(rng, lo=None, hi=None, front=False):
    n = counts(rng, [3 * T // 8] * N if lo is None else lo, [KP] * N if hi is None else hi)
    k = [np.arange(m) if front else np.sort(rng.choice(T, m, replace=False)) for m in n]
    s, p = slots(k)
    return {"kept": np.stack([table(np.concatenate([a, np.full(KP - len(a), -1)])) for a in k]), "snd": s, "pl": p}
def setup_inputs(rng):
    return {"x": f(rng, N, 128, 4 * T), "qw": f(rng, N, 128, QT * 512), **lists(rng)}
def setup_inputs_few(rng):
    return {**setup_inputs(rng), **lists(rng, [T // 2] * (N - 1) + [1], [KP] * (N - 1) + [N])}
def setup_inputs_front(rng):
    return {**setup_inputs(rng), **lists(rng, front=True)}
def setup_inputs_none(rng):
    return {**setup_inputs(rng), **lists(rng, [0] + [T // 2] * (N - 1), [0] + [KP] * (N - 1))}
def setup_inputs_spread(rng):
    d = setup_inputs(rng); d["x"] = wide(rng, N, 128, 4 * T); return d
def setup_inputs_steep(rng):
    d = {**setup_inputs(rng), **lists(rng, [KP] * 5 + [CW + 1, 1, 1], [KP] * 5 + [CW + N, KP, KP])}
    assert (int((d["kept"][:6] >= 0).sum()) - 1) // N - 5 * (CW // N) == DR + CAPP
    return d
def check_inputs(d):
    b, k = [], []
    for q in range(N):
        e = entries(d["kept"][q]); n = int((e >= 0).sum()); k.append(e[:n])
        if e.min() < -1 or e.max() >= T or (e[:n] < 0).any() or (e[n:] != -1).any() or (np.diff(e[:n]) <= 0).any(): b.append("kept")
    if sum(len(a) for a in k) != TOT: b.append("sum of n_q")
    if b: return b
    g = 0
    for q in range(N):
        a = np.arange(g, g + len(k[q])); g += len(k[q])
        if len(a) == 0: continue
        if np.bincount(a % N).max() > CAPP: b.append("columns of a pair")
        p = a // N - q * TOT // (N * N)
        if p.min() < -DR or p.max() > DR + CAPP: b.append("drift")
    s, p = slots(k)
    if not np.array_equal(s, d["snd"]): b.append("snd")
    if not np.array_equal(p, d["pl"]): b.append("pl")
    return b
def reference(x, qw, kept, snd, pl):
    v = []
    for q in range(N):
        e = entries(kept[q]); v.append(cols(x[q], e[e >= 0]))
    v = np.concatenate(v, axis=1)
    y = np.zeros((N, 128, QT * CW), np.float32)
    for r in range(N):
        C = mx_ref.quantize(cols(v, np.arange(r, TOT, N)))
        for o in range(QT): y[r][:, CW * o:CW * o + CW] = mx_ref.matmul(mx_ref.quantize(qw[r][:, 512 * o:512 * o + 512]), C)
    return {"y": y}

@@ -1,0 +1,322 @@
+from concourse.bass import DstId, RemoteDMATransfer
+from concourse.mybir import dt, AluOpType, ActivationFunctionType
+
+N = 8
+KP = 160
+CAPP = KP // N
+CW = 128
+QT = 8
+LC = 3
+HC = 16 * LC
+PADF = 128 - 2 * HC
+PADN = 128 - CAPP
+NE = 128 + (N - 1) * CAPP
+PIECES = [(0, 4), (4, 6), (6, 8)]
+
+SCRATCH = {
+    "L": ("sbuf", [128, KP // 16], "int32"),
+    "UF": ("sbuf", [128, 8 * LC], "uint16"),
+    "UN": ("sbuf", [128, 8 * LC], "uint16"),
+    "X": ("sbuf", [128, 1024], "bfloat16"),
+    "HF": ("sbuf", [128, 4 * (PADF + 2 * HC)], "bfloat16"),
+    "HN": ("sbuf", [128, 4 * (PADN + 2 * HC)], "bfloat16"),
+    "WQ": ("sbuf", [128, QT * 512], "bfloat16"),
+    "WC": ("sbuf", [128, QT * 128], "float8_e4m3fn_x4"),
+    "WS": ("sbuf", [128, QT * 128], "uint8"),
+    "FC": ("sbuf", [128, 128], "float8_e4m3fn_x4"),
+    "FS": ("sbuf", [128, 128], "uint8"),
+    "NC": ("sbuf", [128, 128], "float8_e4m3fn_x4"),
+    "NS": ("sbuf", [128, 128], "uint8"),
+    "EC": ("sbuf", [128, NE], "float8_e4m3fn_x4"),
+    "ES": ("sbuf", [128, NE], "uint8"),
+    "RC": ("sbuf", [128, 2 * CAPP], "float8_e4m3fn_x4"),
+    "RS": ("sbuf", [128, 2 * CAPP], "uint8"),
+    "PLI": ("sbuf", [128, CW // 16], "int32"),
+    "TM": ("sbuf", [128, N * (CW // 16)], "int32"),
+    "AC": ("sbuf", [128, (N + 1) * (CW // 16)], "int32"),
+    "V": ("sbuf", [128, CW // 16], "uint16"),
+    "S": ("sbuf", [128, QT * KP], "float32"),
+    "YS": ("sbuf", [128, QT * CW], "float32"),
+    "P": ("psum", [128, QT * 512], "float32"),
+}
+SEMAPHORES = ["lst", "xin", "q0", "q1", "q2", "pls", "vz", "vy", "vl", "vn", "vg", "sg", "hg", "tg", "qf", "qn", "ex", "wq", "vp",
+              "loc", "near", "far", "rc", "rs", "em", "ec", "lm", "vc", "sc", "vo", "so", "pv", "st"]
+
+
+def by_chip(T, topo, ranks):
+    groups = []
+    for q in sorted(ranks):
+        if groups and T.cores[q] in topo.cores_of(T.cores[groups[-1][-1]]):
+            groups[-1].append(q)
+        else:
+            groups.append([q])
+    return groups
+
+
+def near_far(T, topo, core):
+    near = [q for q in range(N) if T.cores[q] != core and topo.may_write(core, T.cores[q])]
+    far = [q for q in range(N) if T.cores[q] != core and q not in near]
+    here = [q for q in range(N) if T.cores[q] in topo.cores_of(core)]
+    return near, far, here
+
+
+def part(e, i, n):
+    w = len(e) // n
+    return e[i * w:(i + 1) * w]
+
+
+def ports(T, topo, core):
+    near, far, here = near_far(T, topo, core)
+    own = [k for k in topo.cores_of(core) if T.rank_of(k) is None and topo.may_write(k, T.cores[far[0]])]
+    away = [q for q in near if topo.same_plane(core, T.cores[q])]
+    outer = topo.engines(core, T.cores[away[0]])
+    inner = [e for e in topo.engines(core, own[0]) if e not in outer]
+    mine = [k for k in own if topo.die(k) == topo.die(core)]
+    groups = by_chip(T, topo, far)
+    planes = [(mine[i], gr, part(inner, i, len(groups))) for i, gr in enumerate(groups)]
+    codes, taken = [], []
+    for i, q in enumerate(far):
+        port = [k for k in own if topo.die(k) == topo.die(T.cores[q]) and k not in taken][0]
+        taken.append(port)
+        codes.append((port, q, part(inner, i, len(far))))
+    return planes, codes
+
+
+def bits(engines):
+    return sum(1 << e for e in engines)
+
+
+def send(topo, src, dst, engines, sem, frm, to):
+    rid, pid = topo.addr(dst, src)
+    return RemoteDMATransfer(dst_ids=[DstId(rid=rid, pnc=pid)], dma_engine_mask=bits(engines), remote_sem=sem, src=frm, dst=to)
+
+
+def rank_program(g, core, T, topo):
+    rank = T.rank_of(core)
+    if rank is not None:
+        owner_program(g, core, T, topo, rank)
+        return
+    owners = [c for c in T.cores if c in topo.cores_of(core)]
+    if owners and any(core == r[0] for r in ports(T, topo, owners[0])[1]):
+        relay_program(g, core, T, topo, owners)
+
+
+def landing(T, topo, d, src):
+    near, far, here = near_far(T, topo, d)
+    return 128 + (len(near) + far.index(src)) * CAPP
+
+
+def relay_program(g, core, T, topo, owners):
+    M = T.sem
+    planes, codes, wp, wc, left = [], [], 0, 0, 0
+    for c in owners:
+        src = T.rank_of(c)
+        pl, co = ports(T, topo, c)
+        for port, gr, e in pl:
+            if port == core:
+                wp += len(e)
+                for i, q in enumerate(gr):
+                    d = T.cores[q]
+                    a, b = i * CAPP, landing(T, topo, d, src)
+                    es = part(topo.engines(core, d), i, len(gr))
+                    left += len(es)
+                    planes.append(send(topo, core, d, es, M.far, T.RS[:, a:a + CAPP], T.ES[:, b:b + CAPP]))
+        for port, q, e in co:
+            if port == core:
+                wc += len(e)
+                d = T.cores[q]
+    n, b = len(owners) * CAPP, landing(T, topo, d, T.rank_of(owners[0]))
+    es = topo.engines(core, d)
+    codes.append(send(topo, core, d, es, M.far, T.RC[:, 0:n].bitcast(dt.uint8), T.EC[:, b:b + n].bitcast(dt.uint8)))
+    g.wait_ge(M.rs, wp)
+    g.remote_dma_fused(planes, local_sem=M.loc)
+    g.wait_ge(M.rc, wc)
+    g.remote_dma_fused(codes, local_sem=M.loc)
+    g.wait_ge(M.loc, left + len(es))
+
+
+def far_increments(T, topo, core, rank):
+    far = near_far(T, topo, core)[1]
+    n = 0
+    for q in far:
+        pl, co = ports(T, topo, T.cores[q])
+        for port, gr, e in pl:
+            if rank in gr:
+                n += len(part(topo.engines(port, core), gr.index(rank), len(gr)))
+    for gr in by_chip(T, topo, far):
+        n += sum(len(topo.engines(port, core)) for port, q, e in ports(T, topo, T.cores[gr[0]])[1] if q == rank)
+    return n
+
+
+def owner_program(g, core, T, topo, rank):
+    M = T.sem
+    near, far, here = near_far(T, topo, core)
+    fgr = by_chip(T, topo, far)
+    ngr = by_chip(T, topo, near + [rank])
+    K = 2 * LC
+    J = CW // 16
+    COPY = ActivationFunctionType.Copy
+
+    def first(gr):
+        return gr[0] * CAPP // 16
+
+    def place(gs, pad, q):
+        i = [k for k, gr in enumerate(gs) if q in gr][0]
+        return pad + HC * i + q * CAPP - 16 * first(gs[i])
+
+    for p in range(8):
+        q = g.sync if p < 4 else g.scalar
+        q.dma_start(T.L[16 * p:16 * p + 16, :], T.snd[:, :]).then_inc(M.lst, 16)
+    g.sync.dma_start(T.X[:, :], T.x[:, :]).then_inc(M.xin, 16)
+    for k, (a, b) in enumerate(PIECES):
+        g.sync.dma_start(T.WQ[:, 512 * a:512 * b], T.qw[:, 512 * a:512 * b]).then_inc(M["q%d" % k], 16)
+    for p in range(8):
+        g.sync.dma_start(T.PLI[16 * p:16 * p + 16, :], T.pl[:, :]).then_inc(M.pls, 16)
+
+    g.vector.memset(T.HF[:, 0:4 * PADF], 0.0).then_inc(M.vz, 1)
+    g.vector.memset(T.HN[:, 0:4 * PADN], 0.0).then_inc(M.vy, 1)
+
+    def lists(U, gs, sem):
+        for i, gr in enumerate(gs):
+            c = first(gr)
+            g.vector.tensor_scalar(U[:, LC * i:LC * i + LC], T.L[:, c:c + LC], 4, None, AluOpType.mult).then_inc(sem, 1)
+        g.vector.wait_ge(sem, 2)
+        for t in (2, 1, 3):
+            g.vector.tensor_scalar(U[:, K * t:K * t + K], U[:, 0:K], t, None, AluOpType.add).then_inc(sem, 1)
+
+    def gathers(U, H, pad, lsem, vsem, ssem):
+        h0, h1 = 4 * pad, 4 * (pad + 2 * HC)
+        for i, t in enumerate((0, 2)):
+            g.scalar.wait_ge(lsem, 2 + i)
+            g.scalar.activation(H[:, h0 + t:h1:4], T.X[:, 0:1024].indirect(U[:, K * t:K * t + K]), COPY).then_inc(ssem, 1)
+        for i, t in enumerate((1, 3)):
+            g.vector.wait_ge(lsem, 4 + i)
+            g.vector.tensor_copy(H[:, h0 + t:h1:4], T.X[:, 0:1024].indirect(U[:, K * t:K * t + K])).then_inc(vsem, 1)
+        g.vector.wait_ge(vsem, 2)
+        g.vector.wait_ge(ssem, 2)
+
+    g.vector.wait_ge(M.lst, 128)
+    lists(T.UF, fgr, M.vl)
+    g.scalar.wait_ge(M.xin, 16)
+    g.vector.wait_ge(M.xin, 16)
+    gathers(T.UF, T.HF, PADF, M.vl, M.vg, M.sg)
+    g.vector.wait_ge(M.vz, 1)
+    g.vector.quantize_mx(T.FC[:, 0:128], T.FS[:, 0:128], T.HF[:, 0:512]).then_inc(M.qf, 1)
+
+    lists(T.UN, ngr, M.vn)
+    gathers(T.UN, T.HN, PADN, M.vn, M.hg, M.tg)
+    g.vector.wait_ge(M.vy, 1)
+    n0 = PADN + 2 * HC - 128
+    g.vector.quantize_mx(T.NC[:, 0:128], T.NS[:, 0:128], T.HN[:, 4 * n0:4 * n0 + 512]).then_inc(M.qn, 1)
+    s0 = 4 * (place(ngr, PADN, rank) + CAPP - 128)
+    g.vector.quantize_mx(T.EC[:, 0:128], T.ES[:, 0:128], T.HN[:, s0:s0 + 512]).then_inc(M.ex, 1)
+
+    fc, fs, nc, ns = [], [], [], []
+    sent = 0
+    planes, codes = ports(T, topo, core)
+    for port, gr, e in planes:
+        a, n = place(fgr, PADF, gr[0]), len(gr) * CAPP
+        sent += len(e)
+        fs.append(send(topo, core, port, e, M.rs, T.FS[:, a:a + n], T.RS[:, 0:n]))
+    r0 = here.index(rank) * CAPP
+    for port, q, e in codes:
+        a = place(fgr, PADF, q)
+        sent += len(e)
+        fc.append(send(topo, core, port, e, M.rc, T.FC[:, a:a + CAPP].bitcast(dt.uint8), T.RC[:, r0:r0 + CAPP].bitcast(dt.uint8)))
+    away = [q for q in near if topo.same_plane(core, T.cores[q])]
+    landed = 0
+    for q in near:
+        d = T.cores[q]
+        if q in away:
+            e = part(topo.engines(core, d), away.index(q), len(away))
+        else:
+            e = [k for k in topo.engines(core, d) if k not in topo.engines(core, T.cores[away[0]])]
+        landed += 2 * len(e)
+        a, b = place(ngr, PADN, q) - n0, 128 + near_far(T, topo, d)[0].index(rank) * CAPP
+        nc.append(send(topo, core, d, e, M.near, T.NC[:, a:a + CAPP].bitcast(dt.uint8), T.EC[:, b:b + CAPP].bitcast(dt.uint8)))
+        ns.append(send(topo, core, d, e, M.near, T.NS[:, a:a + CAPP], T.ES[:, b:b + CAPP]))
+    g.wait_ge(M.qf, 1)
+    g.remote_dma_fused(fs, local_sem=M.loc)
+    g.remote_dma_fused(fc, local_sem=M.loc)
+    g.wait_ge(M.qn, 1)
+    g.remote_dma_fused(nc, local_sem=M.loc)
+    g.remote_dma_fused(ns, local_sem=M.loc)
+    g.wait_ge(M.loc, sent + landed)
+
+    for k, (a, b) in enumerate(PIECES):
+        g.vector.wait_ge(M["q%d" % k], 16)
+        g.vector.quantize_mx(T.WC[:, 128 * a:128 * b], T.WS[:, 128 * a:128 * b], T.WQ[:, 512 * a:512 * b]).then_inc(M.wq, 1)
+
+    order = [rank] + near + far
+    delta = [CAPP * (order.index(q) - q) for q in range(N)]
+    steps = [(q, delta[q] - delta[q - 1]) for q in range(1, N) if delta[q] != delta[q - 1]]
+    g.vector.wait_ge(M.pls, 128)
+    g.vector.tensor_scalar(T.AC[:, 0:J], T.PLI[:, :], delta[0], None, AluOpType.add).then_inc(M.vp, 1)
+    for i, (q, s) in enumerate(steps):
+        g.vector.tensor_scalar(T.TM[:, J * i:J * i + J], T.PLI[:, :], q * CAPP, s, AluOpType.is_ge, AluOpType.mult).then_inc(M.vp, 1)
+    n = 1 + len(steps)
+    for i in range(len(steps)):
+        g.vector.wait_ge(M.vp, n)
+        g.vector.tensor_tensor(T.AC[:, J * (i + 1):J * (i + 2)], T.AC[:, J * i:J * (i + 1)], T.TM[:, J * i:J * i + J],
+                               AluOpType.add).then_inc(M.vp, 1)
+        n += 1
+    g.vector.wait_ge(M.vp, n)
+    g.vector.tensor_copy(T.V[:, 0:J], T.AC[:, J * len(steps):J * (len(steps) + 1)]).then_inc(M.pv, 1)
+
+    e0 = len(near) * CAPP
+    l0 = NE - 128
+    hw = (1 + len(near)) * CAPP
+    fw = len(far) * CAPP
+
+    def product(o, c0, sem):
+        g.tensor.matmul_mx(T.P[:, 512 * o:512 * o + 128], T.WC[:, 128 * o:128 * o + 128], T.WS[:, 128 * o:128 * o + 128],
+                           T.EC[:, c0:c0 + 128], T.ES[:, c0:c0 + 128], True, True).then_inc(sem, 1)
+    g.tensor.wait_ge(M.ex, 1)
+    g.tensor.wait_ge(M.near, landed)
+    for k in range(len(PIECES)):
+        g.tensor.wait_ge(M.wq, k + 1)
+        for o in range(*PIECES[k]):
+            product(o, e0, M.em)
+            g.scalar.wait_ge(M.em, o + 1)
+            g.scalar.activation(T.S[:, KP * o:KP * o + hw], T.P[:, 512 * o + 128 - hw:512 * o + 128], COPY).then_inc(M.ec, 1)
+    g.tensor.wait_ge(M.far, far_increments(T, topo, core, rank))
+    for o in range(QT):
+        g.tensor.wait_ge(M.ec, o + 1)
+        product(o, l0, M.lm)
+
+    g.vector.wait_ge(M.pv, 1)
+    g.scalar.wait_ge(M.pv, 1)
+    g.scalar.wait_ge(M.ec, QT)
+
+    def copy(o, e):
+        src, dst = T.P[:, 512 * o + 128 - fw:512 * o + 128], T.S[:, KP * o + hw:KP * o + KP]
+        e.wait_ge(M.lm, o + 1)
+        if e is g.scalar:
+            e.activation(dst, src, COPY).then_inc(M.sc, 1)
+        else:
+            e.wait_ge(M.ec, o + 1)
+            e.tensor_copy(dst, src).then_inc(M.vc, 1)
+
+    def pick(o, sem, n):
+        win = T.S[:, KP * o:KP * o + KP].indirect(T.V[:, 0:J])
+        yo = T.YS[:, CW * o:CW * o + CW]
+        if o % 2 == 0:
+            g.vector.wait_ge(sem, n)
+            g.vector.tensor_copy(yo, win).then_inc(M.vo, 1)
+        else:
+            g.scalar.wait_ge(sem, n)
+            g.scalar.activation(yo, win, COPY).then_inc(M.so, 1)
+    for i in range(QT // 2 - 1):
+        copy(2 * i, g.vector)
+        pick(2 * i, M.vc, i + 1)
+        copy(2 * i + 1, g.scalar)
+        pick(2 * i + 1, M.sc, i + 1)
+    copy(QT - 2, g.vector)
+    copy(QT - 1, g.vector)
+    pick(QT - 2, M.vc, QT // 2)
+    pick(QT - 1, M.vc, QT // 2 + 1)
+    for i in range(QT // 2):
+        g.sync.wait_ge(M.vo, i + 1)
+        g.sync.wait_ge(M.so, i + 1)
+        g.sync.dma_start(T.y[:, 2 * CW * i:2 * CW * (i + 1)], T.YS[:, 2 * CW * i:2 * CW * (i + 1)]).then_inc(M.st, 16)
+    g.sync.wait_ge(M.st, 64)

@@ -14,7 +14,7 @@ NE = 128 + (N - 1) * CAPP
 PIECES = [(0, 4), (4, 6), (6, 8)]
 
 SCRATCH = {
-    "L": ("sbuf", [128, KP // 16], "int32"),
+    "L": ("sbuf", [128, 2, KP // 32], "int32"),
     "UF": ("sbuf", [128, 8 * LC], "uint16"),
     "UN": ("sbuf", [128, 8 * LC], "uint16"),
     "X": ("sbuf", [128, 1024], "bfloat16"),
@@ -33,13 +33,13 @@ SCRATCH = {
     "RS": ("sbuf", [128, 2 * CAPP], "uint8"),
     "PLI": ("sbuf", [128, CW // 16], "int32"),
     "TM": ("sbuf", [128, N * (CW // 16)], "int32"),
-    "AC": ("sbuf", [128, (N + 1) * (CW // 16)], "int32"),
-    "V": ("sbuf", [128, CW // 16], "uint16"),
+    "AC": ("sbuf", [128, (N + 2) * (CW // 16)], "int32"),
+    "V": ("sbuf", [128, 2 * CW // 16], "uint16"),
     "S": ("sbuf", [128, QT * KP], "float32"),
     "YS": ("sbuf", [128, QT * CW], "float32"),
     "P": ("psum", [128, QT * 512], "float32"),
 }
-SEMAPHORES = ["lst", "xin", "q0", "q1", "q2", "pls", "vz", "vy", "vl", "vn", "vg", "sg", "hg", "tg", "qf", "qn", "ex", "wq", "vp",
+SEMAPHORES = ["lst", "lr", "xin", "q0", "q1", "q2", "pls", "vz", "vy", "vl", "vn", "vg", "sg", "hg", "tg", "qf", "qn", "ex", "wq", "vp",
               "loc", "near", "far", "rc", "rs", "em", "ec", "lm", "vc", "sc", "vo", "so", "pv", "st"]
 
 
@@ -78,7 +78,7 @@ def ports(T, topo, core):
     for i, q in enumerate(far):
         port = [k for k in own if topo.die(k) == topo.die(T.cores[q]) and k not in taken][0]
         taken.append(port)
-        codes.append((port, q, part(inner, i, len(far))))
+        codes.append((port, q, part(topo.engines(core, port), i, len(far))))
     return planes, codes
 
 
@@ -164,46 +164,46 @@ def owner_program(g, core, T, topo, rank):
         i = [k for k, gr in enumerate(gs) if q in gr][0]
         return pad + HC * i + q * CAPP - 16 * first(gs[i])
 
-    for p in range(8):
-        q = g.sync if p < 4 else g.scalar
-        q.dma_start(T.L[16 * p:16 * p + 16, :], T.snd[:, :]).then_inc(M.lst, 16)
+    for p, q in enumerate((g.sync, g.scalar)):
+        q.dma_start(T.L[16 * p:16 * p + 16, :, :], T.snd[:, :]).then_inc(M.lst, 16)
     g.sync.dma_start(T.X[:, :], T.x[:, :]).then_inc(M.xin, 16)
+    for p in range(2):
+        g.sync.dma_start(T.PLI[16 * p:16 * p + 16, :], T.pl[:, :]).then_inc(M.pls, 16)
     for k, (a, b) in enumerate(PIECES):
         g.sync.dma_start(T.WQ[:, 512 * a:512 * b], T.qw[:, 512 * a:512 * b]).then_inc(M["q%d" % k], 16)
-    for p in range(8):
-        g.sync.dma_start(T.PLI[16 * p:16 * p + 16, :], T.pl[:, :]).then_inc(M.pls, 16)
 
     g.vector.memset(T.HF[:, 0:4 * PADF], 0.0).then_inc(M.vz, 1)
     g.vector.memset(T.HN[:, 0:4 * PADN], 0.0).then_inc(M.vy, 1)
 
     def lists(U, gs, sem):
-        for i, gr in enumerate(gs):
-            c = first(gr)
-            g.vector.tensor_scalar(U[:, LC * i:LC * i + LC], T.L[:, c:c + LC], 4, None, AluOpType.mult).then_inc(sem, 1)
-        g.vector.wait_ge(sem, 2)
-        for t in (2, 1, 3):
-            g.vector.tensor_scalar(U[:, K * t:K * t + K], U[:, 0:K], t, None, AluOpType.add).then_inc(sem, 1)
+        c = first(gs[0])
+        assert first(gs[1]) == c + KP // 32
+        for t in (0, 2, 1, 3):
+            g.vector.tensor_scalar(U[:, K * t:K * t + K], T.L[:, :, c:c + LC], 4, t, AluOpType.mult, AluOpType.add).then_inc(sem, 1)
 
     def gathers(U, H, pad, lsem, vsem, ssem):
         h0, h1 = 4 * pad, 4 * (pad + 2 * HC)
         for i, t in enumerate((0, 2)):
-            g.scalar.wait_ge(lsem, 2 + i)
+            g.scalar.wait_ge(lsem, 1 + i)
             g.scalar.activation(H[:, h0 + t:h1:4], T.X[:, 0:1024].indirect(U[:, K * t:K * t + K]), COPY).then_inc(ssem, 1)
         for i, t in enumerate((1, 3)):
-            g.vector.wait_ge(lsem, 4 + i)
+            g.vector.wait_ge(lsem, 3 + i)
             g.vector.tensor_copy(H[:, h0 + t:h1:4], T.X[:, 0:1024].indirect(U[:, K * t:K * t + K])).then_inc(vsem, 1)
         g.vector.wait_ge(vsem, 2)
         g.vector.wait_ge(ssem, 2)
 
-    g.vector.wait_ge(M.lst, 128)
+    g.vector.wait_ge(M.lst, 32)
+    for p in range(32, 128, 32):
+        g.vector.tensor_copy(T.L[p:p + 32, :, :], T.L[0:32, :, :]).then_inc(M.lr, 1)
+    g.vector.wait_ge(M.lr, 3)
     lists(T.UF, fgr, M.vl)
+    lists(T.UN, ngr, M.vn)
     g.scalar.wait_ge(M.xin, 16)
     g.vector.wait_ge(M.xin, 16)
     gathers(T.UF, T.HF, PADF, M.vl, M.vg, M.sg)
     g.vector.wait_ge(M.vz, 1)
     g.vector.quantize_mx(T.FC[:, 0:128], T.FS[:, 0:128], T.HF[:, 0:512]).then_inc(M.qf, 1)
 
-    lists(T.UN, ngr, M.vn)
     gathers(T.UN, T.HN, PADN, M.vn, M.hg, M.tg)
     g.vector.wait_ge(M.vy, 1)
     n0 = PADN + 2 * HC - 128
@@ -243,25 +243,29 @@ def owner_program(g, core, T, topo, rank):
     g.remote_dma_fused(ns, local_sem=M.loc)
     g.wait_ge(M.loc, sent + landed)
 
-    for k, (a, b) in enumerate(PIECES):
-        g.vector.wait_ge(M["q%d" % k], 16)
-        g.vector.quantize_mx(T.WC[:, 128 * a:128 * b], T.WS[:, 128 * a:128 * b], T.WQ[:, 512 * a:512 * b]).then_inc(M.wq, 1)
-
     order = [rank] + near + far
     delta = [CAPP * (order.index(q) - q) for q in range(N)]
     steps = [(q, delta[q] - delta[q - 1]) for q in range(1, N) if delta[q] != delta[q - 1]]
-    g.vector.wait_ge(M.pls, 128)
-    g.vector.tensor_scalar(T.AC[:, 0:J], T.PLI[:, :], delta[0], None, AluOpType.add).then_inc(M.vp, 1)
+    g.vector.wait_ge(M.pls, 32)
+    g.vector.tensor_scalar(T.AC[0:32, 0:J], T.PLI[0:32, :], delta[0], None, AluOpType.add).then_inc(M.vp, 1)
     for i, (q, s) in enumerate(steps):
-        g.vector.tensor_scalar(T.TM[:, J * i:J * i + J], T.PLI[:, :], q * CAPP, s, AluOpType.is_ge, AluOpType.mult).then_inc(M.vp, 1)
+        g.vector.tensor_scalar(T.TM[0:32, J * i:J * i + J], T.PLI[0:32, :], q * CAPP, s, AluOpType.is_ge, AluOpType.mult).then_inc(M.vp, 1)
     n = 1 + len(steps)
     for i in range(len(steps)):
         g.vector.wait_ge(M.vp, n)
-        g.vector.tensor_tensor(T.AC[:, J * (i + 1):J * (i + 2)], T.AC[:, J * i:J * (i + 1)], T.TM[:, J * i:J * i + J],
+        g.vector.tensor_tensor(T.AC[0:32, J * (i + 1):J * (i + 2)], T.AC[0:32, J * i:J * (i + 1)], T.TM[0:32, J * i:J * i + J],
                                AluOpType.add).then_inc(M.vp, 1)
         n += 1
     g.vector.wait_ge(M.vp, n)
-    g.vector.tensor_copy(T.V[:, 0:J], T.AC[:, J * len(steps):J * (len(steps) + 1)]).then_inc(M.pv, 1)
+    a = J * len(steps)
+    g.vector.tensor_scalar(T.AC[0:32, a + J:a + 2 * J], T.AC[0:32, a:a + J], KP, None, AluOpType.add).then_inc(M.vp, 1)
+    g.vector.wait_ge(M.vp, n + 1)
+    for p in range(0, 128, 32):
+        g.vector.tensor_copy(T.V[p:p + 32, 0:2 * J], T.AC[0:32, a:a + 2 * J]).then_inc(M.pv, 1)
+
+    for k, (a, b) in enumerate(PIECES):
+        g.vector.wait_ge(M["q%d" % k], 16)
+        g.vector.quantize_mx(T.WC[:, 128 * a:128 * b], T.WS[:, 128 * a:128 * b], T.WQ[:, 512 * a:512 * b]).then_inc(M.wq, 1)
 
     e0 = len(near) * CAPP
     l0 = NE - 128
@@ -284,8 +288,8 @@ def owner_program(g, core, T, topo, rank):
         g.tensor.wait_ge(M.ec, o + 1)
         product(o, l0, M.lm)
 
-    g.vector.wait_ge(M.pv, 1)
-    g.scalar.wait_ge(M.pv, 1)
+    g.vector.wait_ge(M.pv, 4)
+    g.scalar.wait_ge(M.pv, 4)
     g.scalar.wait_ge(M.ec, QT)
 
     def copy(o, e):
@@ -297,26 +301,27 @@ def owner_program(g, core, T, topo, rank):
             e.wait_ge(M.ec, o + 1)
             e.tensor_copy(dst, src).then_inc(M.vc, 1)
 
-    def pick(o, sem, n):
-        win = T.S[:, KP * o:KP * o + KP].indirect(T.V[:, 0:J])
-        yo = T.YS[:, CW * o:CW * o + CW]
-        if o % 2 == 0:
-            g.vector.wait_ge(sem, n)
-            g.vector.tensor_copy(yo, win).then_inc(M.vo, 1)
+    def pick(o, e, waits):
+        win = T.S[:, KP * o:KP * (o + 2)].indirect(T.V[:, 0:2 * J])
+        yo = T.YS[:, CW * o:CW * (o + 2)]
+        for sem, n in waits:
+            e.wait_ge(sem, n)
+        if e is g.scalar:
+            e.activation(yo, win, COPY).then_inc(M.so, 1)
         else:
-            g.scalar.wait_ge(sem, n)
-            g.scalar.activation(yo, win, COPY).then_inc(M.so, 1)
-    for i in range(QT // 2 - 1):
-        copy(2 * i, g.vector)
-        pick(2 * i, M.vc, i + 1)
-        copy(2 * i + 1, g.scalar)
-        pick(2 * i + 1, M.sc, i + 1)
-    copy(QT - 2, g.vector)
-    copy(QT - 1, g.vector)
-    pick(QT - 2, M.vc, QT // 2)
-    pick(QT - 1, M.vc, QT // 2 + 1)
+            e.tensor_copy(yo, win).then_inc(M.vo, 1)
+    copy(0, g.vector)
+    copy(1, g.vector)
+    pick(0, g.vector, [(M.vc, 2)])
+    copy(2, g.scalar)
+    copy(3, g.scalar)
+    pick(2, g.scalar, [(M.sc, 2)])
+    for o in (4, 5, 7):
+        copy(o, g.vector)
+    pick(4, g.vector, [(M.vc, 4)])
+    copy(6, g.scalar)
+    pick(6, g.scalar, [(M.sc, 3), (M.vc, 5)])
     for i in range(QT // 2):
-        g.sync.wait_ge(M.vo, i + 1)
-        g.sync.wait_ge(M.so, i + 1)
+        g.sync.wait_ge(M.so if i % 2 else M.vo, i // 2 + 1)
         g.sync.dma_start(T.y[:, 2 * CW * i:2 * CW * (i + 1)], T.YS[:, 2 * CW * i:2 * CW * (i + 1)]).then_inc(M.st, 16)
     g.sync.wait_ge(M.st, 64)

@@ -8,9 +8,10 @@ CW = 128
 QT = 8
 LC = 3
 HC = 16 * LC
-PADF = 128 - 2 * HC
+PADF = 128 - HC + 16
 PADN = 128 - CAPP
 NE = 128 + (N - 1) * CAPP
+BYV = (5, 7)
 PIECES = [(0, 4), (4, 6), (6, 8)]
 
 SCRATCH = {
@@ -18,28 +19,28 @@ SCRATCH = {
     "UF": ("sbuf", [128, 8 * LC], "uint16"),
     "UN": ("sbuf", [128, 8 * LC], "uint16"),
     "X": ("sbuf", [128, 1024], "bfloat16"),
-    "HF": ("sbuf", [128, 4 * (PADF + 2 * HC)], "bfloat16"),
+    "HF": ("sbuf", [128, 4 * (2 * PADF + 2 * HC)], "bfloat16"),
     "HN": ("sbuf", [128, 4 * (PADN + 2 * HC)], "bfloat16"),
     "WQ": ("sbuf", [128, QT * 512], "bfloat16"),
     "WC": ("sbuf", [128, QT * 128], "float8_e4m3fn_x4"),
     "WS": ("sbuf", [128, QT * 128], "uint8"),
-    "FC": ("sbuf", [128, 128], "float8_e4m3fn_x4"),
-    "FS": ("sbuf", [128, 128], "uint8"),
+    "FC": ("sbuf", [128, 256], "float8_e4m3fn_x4"),
+    "FS": ("sbuf", [128, 256], "uint8"),
     "NC": ("sbuf", [128, 128], "float8_e4m3fn_x4"),
     "NS": ("sbuf", [128, 128], "uint8"),
     "EC": ("sbuf", [128, NE], "float8_e4m3fn_x4"),
     "ES": ("sbuf", [128, NE], "uint8"),
     "RC": ("sbuf", [128, 2 * CAPP], "float8_e4m3fn_x4"),
-    "RS": ("sbuf", [128, 2 * CAPP], "uint8"),
+    "RS": ("sbuf", [128, 3 * CAPP], "uint8"),
     "PLI": ("sbuf", [128, CW // 16], "int32"),
     "TM": ("sbuf", [128, N * (CW // 16)], "int32"),
     "AC": ("sbuf", [128, (N + 2) * (CW // 16)], "int32"),
-    "V": ("sbuf", [128, 2 * CW // 16], "uint16"),
+    "V": ("sbuf", [128, 3 * CW // 16], "uint16"),
     "S": ("sbuf", [128, QT * KP], "float32"),
     "YS": ("sbuf", [128, QT * CW], "float32"),
     "P": ("psum", [128, QT * 512], "float32"),
 }
-SEMAPHORES = ["lst", "lr", "xin", "q0", "q1", "q2", "pls", "vz", "vy", "vl", "vn", "vg", "sg", "hg", "tg", "qf", "qn", "ex", "wq", "vp",
+SEMAPHORES = ["rj", "ev", "lst", "lr", "xin", "q0", "q1", "q2", "pls", "vz", "vy", "vl", "vn", "vg", "sg", "hg", "tg", "qf", "qn", "ex", "wq", "vp",
               "loc", "near", "far", "rc", "rs", "em", "ec", "lm", "vc", "sc", "vo", "so", "pv", "st"]
 
 
@@ -65,6 +66,11 @@ def part(e, i, n):
     return e[i * w:(i + 1) * w]
 
 
+def far_chips(T, topo, core):
+    a, b = by_chip(T, topo, near_far(T, topo, core)[1])
+    return [a, b] if topo.host(T.cores[a[0]]) == topo.host(core) else [b[::-1], a]
+
+
 def ports(T, topo, core):
     near, far, here = near_far(T, topo, core)
     own = [k for k in topo.cores_of(core) if T.rank_of(k) is None and topo.may_write(k, T.cores[far[0]])]
@@ -72,14 +78,18 @@ def ports(T, topo, core):
     outer = topo.engines(core, T.cores[away[0]])
     inner = [e for e in topo.engines(core, own[0]) if e not in outer]
     mine = [k for k in own if topo.die(k) == topo.die(core)]
-    groups = by_chip(T, topo, far)
-    planes = [(mine[i], gr, part(inner, i, len(groups))) for i, gr in enumerate(groups)]
+    one, two = far_chips(T, topo, core)
+    planes = [(mine[i], q, inner) for i, q in enumerate(one)]
+    joined = []
+    for i, q in enumerate(two):
+        port = [k for k in own if topo.die(k) == topo.die(T.cores[q])][0]
+        joined.append((port, q, inner[i::2]))
     codes, taken = [], []
     for i, q in enumerate(far):
         port = [k for k in own if topo.die(k) == topo.die(T.cores[q]) and k not in taken][0]
         taken.append(port)
-        codes.append((port, q, part(topo.engines(core, port), i, len(far))))
-    return planes, codes
+        codes.append((port, q, [outer, inner][i // 2][i % 2::2]))
+    return planes, joined, codes
 
 
 def bits(engines):
@@ -96,9 +106,9 @@ def rank_program(g, core, T, topo):
     if rank is not None:
         owner_program(g, core, T, topo, rank)
         return
-    owners = [c for c in T.cores if c in topo.cores_of(core)]
-    if owners and any(core == r[0] for r in ports(T, topo, owners[0])[1]):
-        relay_program(g, core, T, topo, owners)
+    jobs = relay_jobs(T, topo, core)
+    if jobs:
+        relay_program(g, core, T, topo, jobs)
 
 
 def landing(T, topo, d, src):
@@ -106,52 +116,43 @@ def landing(T, topo, d, src):
     return 128 + (len(near) + far.index(src)) * CAPP
 
 
-def relay_program(g, core, T, topo, owners):
+def relay_jobs(T, topo, core):
+    jobs = []
+    for kind in (0, 2, 1):
+        got = [(c, r) for c in T.cores for r in ports(T, topo, c)[kind] if r[0] == core]
+        if got:
+            src, run = got[0]
+            d = T.cores[run[1]]
+            jobs.append((kind, sum(len(r[2]) for c, r in got), d, landing(T, topo, d, T.rank_of(src)), len(got) * CAPP,
+                         topo.engines(core, d)))
+    return jobs
+
+
+def relay_program(g, core, T, topo, jobs):
     M = T.sem
-    planes, codes, wp, wc, left = [], [], 0, 0, 0
-    for c in owners:
-        src = T.rank_of(c)
-        pl, co = ports(T, topo, c)
-        for port, gr, e in pl:
-            if port == core:
-                wp += len(e)
-                for i, q in enumerate(gr):
-                    d = T.cores[q]
-                    a, b = i * CAPP, landing(T, topo, d, src)
-                    es = part(topo.engines(core, d), i, len(gr))
-                    left += len(es)
-                    planes.append(send(topo, core, d, es, M.far, T.RS[:, a:a + CAPP], T.ES[:, b:b + CAPP]))
-        for port, q, e in co:
-            if port == core:
-                wc += len(e)
-                d = T.cores[q]
-    n, b = len(owners) * CAPP, landing(T, topo, d, T.rank_of(owners[0]))
-    es = topo.engines(core, d)
-    codes.append(send(topo, core, d, es, M.far, T.RC[:, 0:n].bitcast(dt.uint8), T.EC[:, b:b + n].bitcast(dt.uint8)))
-    g.wait_ge(M.rs, wp)
-    g.remote_dma_fused(planes, local_sem=M.loc)
-    g.wait_ge(M.rc, wc)
-    g.remote_dma_fused(codes, local_sem=M.loc)
-    g.wait_ge(M.loc, left + len(es))
+    left = 0
+    for kind, n, d, b, w, es in jobs:
+        left += len(es)
+        if kind < 2:
+            tr = send(topo, core, d, es, M.far, T.RS[:, CAPP * kind:CAPP * kind + w], T.ES[:, b:b + w])
+        else:
+            tr = send(topo, core, d, es, M.far, T.RC[:, 0:w].bitcast(dt.uint8), T.EC[:, b:b + w].bitcast(dt.uint8))
+        g.wait_ge([M.rs, M.rj, M.rc][kind], n)
+        g.remote_dma_fused([tr], local_sem=M.loc)
+    g.wait_ge(M.loc, left)
 
 
-def far_increments(T, topo, core, rank):
-    far = near_far(T, topo, core)[1]
-    n = 0
-    for q in far:
-        pl, co = ports(T, topo, T.cores[q])
-        for port, gr, e in pl:
-            if rank in gr:
-                n += len(part(topo.engines(port, core), gr.index(rank), len(gr)))
-    for gr in by_chip(T, topo, far):
-        n += sum(len(topo.engines(port, core)) for port, q, e in ports(T, topo, T.cores[gr[0]])[1] if q == rank)
-    return n
+def far_increments(T, topo, core):
+    helpers = sorted({r[0] for c in T.cores for runs in ports(T, topo, c) for r in runs})
+    return sum(len(job[5]) for k in helpers for job in relay_jobs(T, topo, k) if job[2] == core)
 
 
 def owner_program(g, core, T, topo, rank):
     M = T.sem
     near, far, here = near_far(T, topo, core)
     fgr = by_chip(T, topo, far)
+    lead = far_chips(T, topo, core)[0][0]
+    low = lead == far[0]
     ngr = by_chip(T, topo, near + [rank])
     K = 2 * LC
     J = CW // 16
@@ -160,9 +161,9 @@ def owner_program(g, core, T, topo, rank):
     def first(gr):
         return gr[0] * CAPP // 16
 
-    def place(gs, pad, q):
+    def place(gs, pad, q, step=HC):
         i = [k for k, gr in enumerate(gs) if q in gr][0]
-        return pad + HC * i + q * CAPP - 16 * first(gs[i])
+        return pad + step * i + q * CAPP - 16 * first(gs[i])
 
     for p, q in enumerate((g.sync, g.scalar)):
         q.dma_start(T.L[16 * p:16 * p + 16, :, :], T.snd[:, :]).then_inc(M.lst, 16)
@@ -172,39 +173,76 @@ def owner_program(g, core, T, topo, rank):
     for k, (a, b) in enumerate(PIECES):
         g.sync.dma_start(T.WQ[:, 512 * a:512 * b], T.qw[:, 512 * a:512 * b]).then_inc(M["q%d" % k], 16)
 
-    g.vector.memset(T.HF[:, 0:4 * PADF], 0.0).then_inc(M.vz, 1)
+    z0 = 0 if low else PADF + 2 * HC
+    g.vector.memset(T.HF[:, 4 * z0:4 * (z0 + PADF)], 0.0).then_inc(M.vz, 1)
+    cut = LC - 1 if low else LC + 1
+    wins = (0, 2 * PADF - 128) if low else (PADF + 16 * cut, PADF)
     g.vector.memset(T.HN[:, 0:4 * PADN], 0.0).then_inc(M.vy, 1)
 
-    def lists(U, gs, sem):
-        c = first(gs[0])
-        assert first(gs[1]) == c + KP // 32
-        for t in (0, 2, 1, 3):
-            g.vector.tensor_scalar(U[:, K * t:K * t + K], T.L[:, :, c:c + LC], 4, t, AluOpType.mult, AluOpType.add).then_inc(sem, 1)
-
-    def gathers(U, H, pad, lsem, vsem, ssem):
-        h0, h1 = 4 * pad, 4 * (pad + 2 * HC)
-        for i, t in enumerate((0, 2)):
-            g.scalar.wait_ge(lsem, 1 + i)
-            g.scalar.activation(H[:, h0 + t:h1:4], T.X[:, 0:1024].indirect(U[:, K * t:K * t + K]), COPY).then_inc(ssem, 1)
-        for i, t in enumerate((1, 3)):
-            g.vector.wait_ge(lsem, 3 + i)
-            g.vector.tensor_copy(H[:, h0 + t:h1:4], T.X[:, 0:1024].indirect(U[:, K * t:K * t + K])).then_inc(vsem, 1)
-        g.vector.wait_ge(vsem, 2)
-        g.vector.wait_ge(ssem, 2)
+    def near_lists(ts):
+        c = first(ngr[0])
+        for t in ts:
+            g.vector.tensor_scalar(T.UN[:, K * t:K * t + K], T.L[:, :, c:c + LC], 4, t, AluOpType.mult, AluOpType.add).then_inc(M.vn, 1)
 
     g.vector.wait_ge(M.lst, 32)
     for p in range(32, 128, 32):
         g.vector.tensor_copy(T.L[p:p + 32, :, :], T.L[0:32, :, :]).then_inc(M.lr, 1)
     g.vector.wait_ge(M.lr, 3)
-    lists(T.UF, fgr, M.vl)
-    lists(T.UN, ngr, M.vn)
+    c = first(fgr[0])
+    for t in range(4):
+        g.vector.tensor_scalar(T.UF[:, K * t:K * t + K], T.L[:, :, c:c + LC], 4, t, AluOpType.mult, AluOpType.add).then_inc(M.vl, 1)
     g.scalar.wait_ge(M.xin, 16)
     g.vector.wait_ge(M.xin, 16)
-    gathers(T.UF, T.HF, PADF, M.vl, M.vg, M.sg)
-    g.vector.wait_ge(M.vz, 1)
-    g.vector.quantize_mx(T.FC[:, 0:128], T.FS[:, 0:128], T.HF[:, 0:512]).then_inc(M.qf, 1)
 
-    gathers(T.UN, T.HN, PADN, M.vn, M.hg, M.tg)
+    def far_gather(e, a, b, ts):
+        h0, h1 = 4 * (PADF + 16 * a), 4 * (PADF + 16 * b)
+        for t in ts:
+            e.wait_ge(M.vl, t + 1)
+            win = T.X[:, 0:1024].indirect(T.UF[:, K * t + a:K * t + b])
+            if e is g.scalar:
+                e.activation(T.HF[:, h0 + t:h1:4], win, COPY).then_inc(M.sg, 1)
+            else:
+                e.tensor_copy(T.HF[:, h0 + t:h1:4], win).then_inc(M.vg, 1)
+
+    def far_codes(i, n):
+        g.vector.wait_ge(M.vg, n)
+        g.vector.wait_ge(M.sg, n)
+        g.vector.quantize_mx(T.FC[:, 128 * i:128 * i + 128], T.FS[:, 128 * i:128 * i + 128],
+                             T.HF[:, 4 * wins[i]:4 * wins[i] + 512]).then_inc(M.qf, 1)
+    head, rest = [(0, cut), (cut, K)] if low else [(cut, K), (0, cut)]
+    far_gather(g.scalar, *head, (0, 2))
+    far_gather(g.scalar, *rest, (0, 2))
+    far_gather(g.vector, *head, (1, 3))
+    near_lists((0, 1))
+    far_gather(g.vector, *rest, (1,))
+    g.vector.wait_ge(M.vz, 1)
+    far_codes(0, 2)
+    far_gather(g.vector, *rest, (3,))
+    near_lists((2, 3))
+    far_codes(1, 4)
+
+    def far_place(q):
+        a = place(fgr, PADF, q)
+        return a - wins[0] if q == lead else a - wins[1] + 128
+
+    h0, h1 = 4 * PADN, 4 * (PADN + 2 * HC)
+    for t in range(4):
+        win = T.X[:, 0:1024].indirect(T.UN[:, K * t:K * t + K])
+        if t < 3:
+            g.scalar.wait_ge(M.vn, t + 1)
+            g.scalar.activation(T.HN[:, h0 + t:h1:4], win, COPY).then_inc(M.tg, 1)
+        else:
+            g.vector.wait_ge(M.vn, t + 1)
+            g.vector.tensor_copy(T.HN[:, h0 + t:h1:4], win).then_inc(M.hg, 1)
+    order = [rank] + near + far
+    delta = [CAPP * (order.index(q) - q) for q in range(N)]
+    steps = [(q, delta[q] - delta[q - 1]) for q in range(1, N) if delta[q] != delta[q - 1]]
+    g.vector.wait_ge(M.pls, 32)
+    g.vector.tensor_scalar(T.AC[0:32, 0:J], T.PLI[0:32, :], delta[0], None, AluOpType.add).then_inc(M.vp, 1)
+    for i, (q, s) in enumerate(steps):
+        g.vector.tensor_scalar(T.TM[0:32, J * i:J * i + J], T.PLI[0:32, :], q * CAPP, s, AluOpType.is_ge, AluOpType.mult).then_inc(M.vp, 1)
+    g.vector.wait_ge(M.hg, 1)
+    g.vector.wait_ge(M.tg, 3)
     g.vector.wait_ge(M.vy, 1)
     n0 = PADN + 2 * HC - 128
     g.vector.quantize_mx(T.NC[:, 0:128], T.NS[:, 0:128], T.HN[:, 4 * n0:4 * n0 + 512]).then_inc(M.qn, 1)
@@ -213,14 +251,19 @@ def owner_program(g, core, T, topo, rank):
 
     fc, fs, nc, ns = [], [], [], []
     sent = 0
-    planes, codes = ports(T, topo, core)
-    for port, gr, e in planes:
-        a, n = place(fgr, PADF, gr[0]), len(gr) * CAPP
+    planes, joined, codes = ports(T, topo, core)
+    for port, q, e in planes:
+        a = far_place(q)
         sent += len(e)
-        fs.append(send(topo, core, port, e, M.rs, T.FS[:, a:a + n], T.RS[:, 0:n]))
+        fs.append(send(topo, core, port, e, M.rs, T.FS[:, a:a + CAPP], T.RS[:, 0:CAPP]))
     r0 = here.index(rank) * CAPP
+    fj = []
+    for port, q, e in joined:
+        a = far_place(q)
+        sent += len(e)
+        fj.append(send(topo, core, port, e, M.rj, T.FS[:, a:a + CAPP], T.RS[:, CAPP + r0:2 * CAPP + r0]))
     for port, q, e in codes:
-        a = place(fgr, PADF, q)
+        a = far_place(q)
         sent += len(e)
         fc.append(send(topo, core, port, e, M.rc, T.FC[:, a:a + CAPP].bitcast(dt.uint8), T.RC[:, r0:r0 + CAPP].bitcast(dt.uint8)))
     away = [q for q in near if topo.same_plane(core, T.cores[q])]
@@ -235,37 +278,32 @@ def owner_program(g, core, T, topo, rank):
         a, b = place(ngr, PADN, q) - n0, 128 + near_far(T, topo, d)[0].index(rank) * CAPP
         nc.append(send(topo, core, d, e, M.near, T.NC[:, a:a + CAPP].bitcast(dt.uint8), T.EC[:, b:b + CAPP].bitcast(dt.uint8)))
         ns.append(send(topo, core, d, e, M.near, T.NS[:, a:a + CAPP], T.ES[:, b:b + CAPP]))
-    g.wait_ge(M.qf, 1)
-    g.remote_dma_fused(fs, local_sem=M.loc)
+    for i, tr in enumerate(fs):
+        g.wait_ge(M.qf, i + 1)
+        g.remote_dma_fused([tr], local_sem=M.loc)
     g.remote_dma_fused(fc, local_sem=M.loc)
+    g.remote_dma_fused(fj, local_sem=M.loc)
     g.wait_ge(M.qn, 1)
     g.remote_dma_fused(nc, local_sem=M.loc)
     g.remote_dma_fused(ns, local_sem=M.loc)
     g.wait_ge(M.loc, sent + landed)
 
-    order = [rank] + near + far
-    delta = [CAPP * (order.index(q) - q) for q in range(N)]
-    steps = [(q, delta[q] - delta[q - 1]) for q in range(1, N) if delta[q] != delta[q - 1]]
-    g.vector.wait_ge(M.pls, 32)
-    g.vector.tensor_scalar(T.AC[0:32, 0:J], T.PLI[0:32, :], delta[0], None, AluOpType.add).then_inc(M.vp, 1)
-    for i, (q, s) in enumerate(steps):
-        g.vector.tensor_scalar(T.TM[0:32, J * i:J * i + J], T.PLI[0:32, :], q * CAPP, s, AluOpType.is_ge, AluOpType.mult).then_inc(M.vp, 1)
     n = 1 + len(steps)
-    for i in range(len(steps)):
-        g.vector.wait_ge(M.vp, n)
-        g.vector.tensor_tensor(T.AC[0:32, J * (i + 1):J * (i + 2)], T.AC[0:32, J * i:J * (i + 1)], T.TM[0:32, J * i:J * i + J],
-                               AluOpType.add).then_inc(M.vp, 1)
-        n += 1
-    g.vector.wait_ge(M.vp, n)
+    for i in range(QT // 2):
+        if i < len(steps):
+            g.vector.wait_ge(M.vp, n + i)
+            g.vector.tensor_tensor(T.AC[0:32, J * (i + 1):J * (i + 2)], T.AC[0:32, J * i:J * (i + 1)], T.TM[0:32, J * i:J * i + J],
+                                   AluOpType.add).then_inc(M.vp, 1)
+        a, b = 2 * i, 2 * i + 2
+        g.vector.wait_ge(M["q%d" % [k for k, pc in enumerate(PIECES) if pc[0] <= a < pc[1]][0]], 16)
+        g.vector.quantize_mx(T.WC[:, 128 * a:128 * b], T.WS[:, 128 * a:128 * b], T.WQ[:, 512 * a:512 * b]).then_inc(M.wq, 1)
+    assert len(steps) <= QT // 2
+    g.vector.wait_ge(M.vp, n + len(steps))
     a = J * len(steps)
     g.vector.tensor_scalar(T.AC[0:32, a + J:a + 2 * J], T.AC[0:32, a:a + J], KP, None, AluOpType.add).then_inc(M.vp, 1)
-    g.vector.wait_ge(M.vp, n + 1)
+    g.vector.wait_ge(M.vp, n + len(steps) + 1)
     for p in range(0, 128, 32):
         g.vector.tensor_copy(T.V[p:p + 32, 0:2 * J], T.AC[0:32, a:a + 2 * J]).then_inc(M.pv, 1)
-
-    for k, (a, b) in enumerate(PIECES):
-        g.vector.wait_ge(M["q%d" % k], 16)
-        g.vector.quantize_mx(T.WC[:, 128 * a:128 * b], T.WS[:, 128 * a:128 * b], T.WQ[:, 512 * a:512 * b]).then_inc(M.wq, 1)
 
     e0 = len(near) * CAPP
     l0 = NE - 128
@@ -277,20 +315,24 @@ def owner_program(g, core, T, topo, rank):
                            T.EC[:, c0:c0 + 128], T.ES[:, c0:c0 + 128], True, True).then_inc(sem, 1)
     g.tensor.wait_ge(M.ex, 1)
     g.tensor.wait_ge(M.near, landed)
-    for k in range(len(PIECES)):
+    for k in range(QT // 2):
         g.tensor.wait_ge(M.wq, k + 1)
-        for o in range(*PIECES[k]):
+        for o in (2 * k, 2 * k + 1):
             product(o, e0, M.em)
-            g.scalar.wait_ge(M.em, o + 1)
-            g.scalar.activation(T.S[:, KP * o:KP * o + hw], T.P[:, 512 * o + 128 - hw:512 * o + 128], COPY).then_inc(M.ec, 1)
-    g.tensor.wait_ge(M.far, far_increments(T, topo, core, rank))
+            src, dst = T.P[:, 512 * o + 128 - hw:512 * o + 128], T.S[:, KP * o:KP * o + hw]
+            if o in BYV:
+                g.vector.wait_ge(M.em, o + 1)
+                g.vector.tensor_copy(dst, src).then_inc(M.ev, 1)
+            else:
+                g.scalar.wait_ge(M.em, o + 1)
+                g.scalar.activation(dst, src, COPY).then_inc(M.ec, 1)
+    g.tensor.wait_ge(M.far, far_increments(T, topo, core))
     for o in range(QT):
-        g.tensor.wait_ge(M.ec, o + 1)
+        g.tensor.wait_ge(M.ev if o in BYV else M.ec, len([k for k in range(o + 1) if (k in BYV) == (o in BYV)]))
         product(o, l0, M.lm)
 
     g.vector.wait_ge(M.pv, 4)
     g.scalar.wait_ge(M.pv, 4)
-    g.scalar.wait_ge(M.ec, QT)
 
     def copy(o, e):
         src, dst = T.P[:, 512 * o + 128 - fw:512 * o + 128], T.S[:, KP * o + hw:KP * o + KP]
@@ -298,30 +340,30 @@ def owner_program(g, core, T, topo, rank):
         if e is g.scalar:
             e.activation(dst, src, COPY).then_inc(M.sc, 1)
         else:
-            e.wait_ge(M.ec, o + 1)
             e.tensor_copy(dst, src).then_inc(M.vc, 1)
 
-    def pick(o, e, waits):
-        win = T.S[:, KP * o:KP * (o + 2)].indirect(T.V[:, 0:2 * J])
-        yo = T.YS[:, CW * o:CW * (o + 2)]
-        for sem, n in waits:
-            e.wait_ge(sem, n)
+    def pick(o, k, e, sem, n):
+        win = T.S[:, KP * o:KP * (o + k)].indirect(T.V[:, 0:k * J])
+        yo = T.YS[:, CW * o:CW * (o + k)]
+        for s, v in ((M.vc, sem), (M.sc, n)):
+            if v:
+                e.wait_ge(s, v)
         if e is g.scalar:
             e.activation(yo, win, COPY).then_inc(M.so, 1)
         else:
             e.tensor_copy(yo, win).then_inc(M.vo, 1)
-    copy(0, g.vector)
-    copy(1, g.vector)
-    pick(0, g.vector, [(M.vc, 2)])
-    copy(2, g.scalar)
-    copy(3, g.scalar)
-    pick(2, g.scalar, [(M.sc, 2)])
-    for o in (4, 5, 7):
+    for o in (0, 2):
         copy(o, g.vector)
-    pick(4, g.vector, [(M.vc, 4)])
-    copy(6, g.scalar)
-    pick(6, g.scalar, [(M.sc, 3), (M.vc, 5)])
-    for i in range(QT // 2):
-        g.sync.wait_ge(M.so if i % 2 else M.vo, i // 2 + 1)
-        g.sync.dma_start(T.y[:, 2 * CW * i:2 * CW * (i + 1)], T.YS[:, 2 * CW * i:2 * CW * (i + 1)]).then_inc(M.st, 16)
-    g.sync.wait_ge(M.st, 64)
+    for o in (1, 3, 4, 5, 6, 7):
+        copy(o, g.scalar)
+    pick(0, 1, g.vector, 1, 0)
+    pick(1, 2, g.vector, 2, 1)
+    pick(3, 1, g.scalar, 0, 2)
+    pick(4, 2, g.vector, 2, 4)
+    pick(6, 2, g.scalar, 0, 6)
+    for a, b, nv, ns in [(0, 1, 1, 0), (1, 4, 2, 1), (4, 8, 3, 2)]:
+        g.sync.wait_ge(M.vo, nv)
+        if ns:
+            g.sync.wait_ge(M.so, ns)
+        g.sync.dma_start(T.y[:, CW * a:CW * b], T.YS[:, CW * a:CW * b]).then_inc(M.st, 16)
+    g.sync.wait_ge(M.st, 48)

from concourse.bass import DstId, RemoteDMATransfer
from concourse.mybir import dt, AluOpType, ActivationFunctionType

N = 8
KP = 160
CAPP = KP // N
CW = 128
QT = 8
LC = 3
HC = 16 * LC
PADF = 128 - HC + 16
PADN = 128 - CAPP
NE = 128 + (N - 1) * CAPP
BYV = (5, 7)
PIECES = [(0, 4), (4, 6), (6, 8)]

SCRATCH = {
    "L": ("sbuf", [128, 2, KP // 32], "int32"),
    "UF": ("sbuf", [128, 8 * LC], "uint16"),
    "UN": ("sbuf", [128, 8 * LC], "uint16"),
    "X": ("sbuf", [128, 1024], "bfloat16"),
    "HF": ("sbuf", [128, 4 * (2 * PADF + 2 * HC)], "bfloat16"),
    "HN": ("sbuf", [128, 4 * (PADN + 2 * HC)], "bfloat16"),
    "WQ": ("sbuf", [128, QT * 512], "bfloat16"),
    "WC": ("sbuf", [128, QT * 128], "float8_e4m3fn_x4"),
    "WS": ("sbuf", [128, QT * 128], "uint8"),
    "FC": ("sbuf", [128, 256], "float8_e4m3fn_x4"),
    "FS": ("sbuf", [128, 256], "uint8"),
    "NC": ("sbuf", [128, 128], "float8_e4m3fn_x4"),
    "NS": ("sbuf", [128, 128], "uint8"),
    "EC": ("sbuf", [128, NE], "float8_e4m3fn_x4"),
    "ES": ("sbuf", [128, NE], "uint8"),
    "RC": ("sbuf", [128, 2 * CAPP], "float8_e4m3fn_x4"),
    "RS": ("sbuf", [128, 3 * CAPP], "uint8"),
    "PLI": ("sbuf", [128, CW // 16], "int32"),
    "TM": ("sbuf", [128, N * (CW // 16)], "int32"),
    "AC": ("sbuf", [128, (N + 2) * (CW // 16)], "int32"),
    "V": ("sbuf", [128, 3 * CW // 16], "uint16"),
    "S": ("sbuf", [128, QT * KP], "float32"),
    "YS": ("sbuf", [128, QT * CW], "float32"),
    "P": ("psum", [128, QT * 512], "float32"),
}
SEMAPHORES = ["rj", "ev", "lst", "lr", "xin", "q0", "q1", "q2", "pls", "vz", "vy", "vl", "vn", "vg", "sg", "hg", "tg", "qf", "qn", "ex", "wq", "vp",
              "loc", "near", "far", "rc", "rs", "em", "ec", "lm", "vc", "sc", "vo", "so", "pv", "st"]


def by_chip(T, topo, ranks):
    groups = []
    for q in sorted(ranks):
        if groups and T.cores[q] in topo.cores_of(T.cores[groups[-1][-1]]):
            groups[-1].append(q)
        else:
            groups.append([q])
    return groups


def near_far(T, topo, core):
    near = [q for q in range(N) if T.cores[q] != core and topo.may_write(core, T.cores[q])]
    far = [q for q in range(N) if T.cores[q] != core and q not in near]
    here = [q for q in range(N) if T.cores[q] in topo.cores_of(core)]
    return near, far, here


def part(e, i, n):
    w = len(e) // n
    return e[i * w:(i + 1) * w]


def far_chips(T, topo, core):
    a, b = by_chip(T, topo, near_far(T, topo, core)[1])
    return [a, b] if topo.host(T.cores[a[0]]) == topo.host(core) else [b[::-1], a]


def ports(T, topo, core):
    near, far, here = near_far(T, topo, core)
    own = [k for k in topo.cores_of(core) if T.rank_of(k) is None and topo.may_write(k, T.cores[far[0]])]
    away = [q for q in near if topo.same_plane(core, T.cores[q])]
    outer = topo.engines(core, T.cores[away[0]])
    inner = [e for e in topo.engines(core, own[0]) if e not in outer]
    mine = [k for k in own if topo.die(k) == topo.die(core)]
    one, two = far_chips(T, topo, core)
    planes = [(mine[i], q, inner) for i, q in enumerate(one)]
    joined = []
    for i, q in enumerate(two):
        port = [k for k in own if topo.die(k) == topo.die(T.cores[q])][0]
        joined.append((port, q, inner[i::2]))
    codes, taken = [], []
    for i, q in enumerate(far):
        port = [k for k in own if topo.die(k) == topo.die(T.cores[q]) and k not in taken][0]
        taken.append(port)
        codes.append((port, q, [outer, inner][i // 2][i % 2::2]))
    return planes, joined, codes


def bits(engines):
    return sum(1 << e for e in engines)


def send(topo, src, dst, engines, sem, frm, to):
    rid, pid = topo.addr(dst, src)
    return RemoteDMATransfer(dst_ids=[DstId(rid=rid, pnc=pid)], dma_engine_mask=bits(engines), remote_sem=sem, src=frm, dst=to)


def rank_program(g, core, T, topo):
    rank = T.rank_of(core)
    if rank is not None:
        owner_program(g, core, T, topo, rank)
        return
    jobs = relay_jobs(T, topo, core)
    if jobs:
        relay_program(g, core, T, topo, jobs)


def landing(T, topo, d, src):
    near, far, here = near_far(T, topo, d)
    return 128 + (len(near) + far.index(src)) * CAPP


def relay_jobs(T, topo, core):
    jobs = []
    for kind in (0, 2, 1):
        got = [(c, r) for c in T.cores for r in ports(T, topo, c)[kind] if r[0] == core]
        if got:
            src, run = got[0]
            d = T.cores[run[1]]
            jobs.append((kind, sum(len(r[2]) for c, r in got), d, landing(T, topo, d, T.rank_of(src)), len(got) * CAPP,
                         topo.engines(core, d)))
    return jobs


def relay_program(g, core, T, topo, jobs):
    M = T.sem
    left = 0
    for kind, n, d, b, w, es in jobs:
        left += len(es)
        if kind < 2:
            tr = send(topo, core, d, es, M.far, T.RS[:, CAPP * kind:CAPP * kind + w], T.ES[:, b:b + w])
        else:
            tr = send(topo, core, d, es, M.far, T.RC[:, 0:w].bitcast(dt.uint8), T.EC[:, b:b + w].bitcast(dt.uint8))
        g.wait_ge([M.rs, M.rj, M.rc][kind], n)
        g.remote_dma_fused([tr], local_sem=M.loc)
    g.wait_ge(M.loc, left)


def far_increments(T, topo, core):
    helpers = sorted({r[0] for c in T.cores for runs in ports(T, topo, c) for r in runs})
    return sum(len(job[5]) for k in helpers for job in relay_jobs(T, topo, k) if job[2] == core)


def owner_program(g, core, T, topo, rank):
    M = T.sem
    near, far, here = near_far(T, topo, core)
    fgr = by_chip(T, topo, far)
    lead = far_chips(T, topo, core)[0][0]
    low = lead == far[0]
    ngr = by_chip(T, topo, near + [rank])
    K = 2 * LC
    J = CW // 16
    COPY = ActivationFunctionType.Copy

    def first(gr):
        return gr[0] * CAPP // 16

    def place(gs, pad, q, step=HC):
        i = [k for k, gr in enumerate(gs) if q in gr][0]
        return pad + step * i + q * CAPP - 16 * first(gs[i])

    for p, q in enumerate((g.sync, g.scalar)):
        q.dma_start(T.L[16 * p:16 * p + 16, :, :], T.snd[:, :]).then_inc(M.lst, 16)
    g.sync.dma_start(T.X[:, :], T.x[:, :]).then_inc(M.xin, 16)
    for p in range(2):
        g.sync.dma_start(T.PLI[16 * p:16 * p + 16, :], T.pl[:, :]).then_inc(M.pls, 16)
    for k, (a, b) in enumerate(PIECES):
        g.sync.dma_start(T.WQ[:, 512 * a:512 * b], T.qw[:, 512 * a:512 * b]).then_inc(M["q%d" % k], 16)

    z0 = 0 if low else PADF + 2 * HC
    g.vector.memset(T.HF[:, 4 * z0:4 * (z0 + PADF)], 0.0).then_inc(M.vz, 1)
    cut = LC - 1 if low else LC + 1
    wins = (0, 2 * PADF - 128) if low else (PADF + 16 * cut, PADF)
    g.vector.memset(T.HN[:, 0:4 * PADN], 0.0).then_inc(M.vy, 1)

    def near_lists(ts):
        c = first(ngr[0])
        for t in ts:
            g.vector.tensor_scalar(T.UN[:, K * t:K * t + K], T.L[:, :, c:c + LC], 4, t, AluOpType.mult, AluOpType.add).then_inc(M.vn, 1)

    g.vector.wait_ge(M.lst, 32)
    for p in range(32, 128, 32):
        g.vector.tensor_copy(T.L[p:p + 32, :, :], T.L[0:32, :, :]).then_inc(M.lr, 1)
    g.vector.wait_ge(M.lr, 3)
    c = first(fgr[0])
    for t in range(4):
        g.vector.tensor_scalar(T.UF[:, K * t:K * t + K], T.L[:, :, c:c + LC], 4, t, AluOpType.mult, AluOpType.add).then_inc(M.vl, 1)
    g.scalar.wait_ge(M.xin, 16)
    g.vector.wait_ge(M.xin, 16)

    def far_gather(e, a, b, ts):
        h0, h1 = 4 * (PADF + 16 * a), 4 * (PADF + 16 * b)
        for t in ts:
            e.wait_ge(M.vl, t + 1)
            win = T.X[:, 0:1024].indirect(T.UF[:, K * t + a:K * t + b])
            if e is g.scalar:
                e.activation(T.HF[:, h0 + t:h1:4], win, COPY).then_inc(M.sg, 1)
            else:
                e.tensor_copy(T.HF[:, h0 + t:h1:4], win).then_inc(M.vg, 1)

    def far_codes(i, n):
        g.vector.wait_ge(M.vg, n)
        g.vector.wait_ge(M.sg, n)
        g.vector.quantize_mx(T.FC[:, 128 * i:128 * i + 128], T.FS[:, 128 * i:128 * i + 128],
                             T.HF[:, 4 * wins[i]:4 * wins[i] + 512]).then_inc(M.qf, 1)
    head, rest = [(0, cut), (cut, K)] if low else [(cut, K), (0, cut)]
    far_gather(g.scalar, *head, (0, 2))
    far_gather(g.scalar, *rest, (0, 2))
    far_gather(g.vector, *head, (1, 3))
    near_lists((0, 1))
    far_gather(g.vector, *rest, (1,))
    g.vector.wait_ge(M.vz, 1)
    far_codes(0, 2)
    far_gather(g.vector, *rest, (3,))
    near_lists((2, 3))
    far_codes(1, 4)

    def far_place(q):
        a = place(fgr, PADF, q)
        return a - wins[0] if q == lead else a - wins[1] + 128

    h0, h1 = 4 * PADN, 4 * (PADN + 2 * HC)
    for t in range(4):
        win = T.X[:, 0:1024].indirect(T.UN[:, K * t:K * t + K])
        if t < 3:
            g.scalar.wait_ge(M.vn, t + 1)
            g.scalar.activation(T.HN[:, h0 + t:h1:4], win, COPY).then_inc(M.tg, 1)
        else:
            g.vector.wait_ge(M.vn, t + 1)
            g.vector.tensor_copy(T.HN[:, h0 + t:h1:4], win).then_inc(M.hg, 1)
    order = [rank] + near + far
    delta = [CAPP * (order.index(q) - q) for q in range(N)]
    steps = [(q, delta[q] - delta[q - 1]) for q in range(1, N) if delta[q] != delta[q - 1]]
    g.vector.wait_ge(M.pls, 32)
    g.vector.tensor_scalar(T.AC[0:32, 0:J], T.PLI[0:32, :], delta[0], None, AluOpType.add).then_inc(M.vp, 1)
    for i, (q, s) in enumerate(steps):
        g.vector.tensor_scalar(T.TM[0:32, J * i:J * i + J], T.PLI[0:32, :], q * CAPP, s, AluOpType.is_ge, AluOpType.mult).then_inc(M.vp, 1)
    g.vector.wait_ge(M.hg, 1)
    g.vector.wait_ge(M.tg, 3)
    g.vector.wait_ge(M.vy, 1)
    n0 = PADN + 2 * HC - 128
    g.vector.quantize_mx(T.NC[:, 0:128], T.NS[:, 0:128], T.HN[:, 4 * n0:4 * n0 + 512]).then_inc(M.qn, 1)
    s0 = 4 * (place(ngr, PADN, rank) + CAPP - 128)
    g.vector.quantize_mx(T.EC[:, 0:128], T.ES[:, 0:128], T.HN[:, s0:s0 + 512]).then_inc(M.ex, 1)

    fc, fs, nc, ns = [], [], [], []
    sent = 0
    planes, joined, codes = ports(T, topo, core)
    for port, q, e in planes:
        a = far_place(q)
        sent += len(e)
        fs.append(send(topo, core, port, e, M.rs, T.FS[:, a:a + CAPP], T.RS[:, 0:CAPP]))
    r0 = here.index(rank) * CAPP
    fj = []
    for port, q, e in joined:
        a = far_place(q)
        sent += len(e)
        fj.append(send(topo, core, port, e, M.rj, T.FS[:, a:a + CAPP], T.RS[:, CAPP + r0:2 * CAPP + r0]))
    for port, q, e in codes:
        a = far_place(q)
        sent += len(e)
        fc.append(send(topo, core, port, e, M.rc, T.FC[:, a:a + CAPP].bitcast(dt.uint8), T.RC[:, r0:r0 + CAPP].bitcast(dt.uint8)))
    away = [q for q in near if topo.same_plane(core, T.cores[q])]
    landed = 0
    for q in near:
        d = T.cores[q]
        if q in away:
            e = part(topo.engines(core, d), away.index(q), len(away))
        else:
            e = [k for k in topo.engines(core, d) if k not in topo.engines(core, T.cores[away[0]])]
        landed += 2 * len(e)
        a, b = place(ngr, PADN, q) - n0, 128 + near_far(T, topo, d)[0].index(rank) * CAPP
        nc.append(send(topo, core, d, e, M.near, T.NC[:, a:a + CAPP].bitcast(dt.uint8), T.EC[:, b:b + CAPP].bitcast(dt.uint8)))
        ns.append(send(topo, core, d, e, M.near, T.NS[:, a:a + CAPP], T.ES[:, b:b + CAPP]))
    for i, tr in enumerate(fs):
        g.wait_ge(M.qf, i + 1)
        g.remote_dma_fused([tr], local_sem=M.loc)
    g.remote_dma_fused(fc, local_sem=M.loc)
    g.remote_dma_fused(fj, local_sem=M.loc)
    g.wait_ge(M.qn, 1)
    g.remote_dma_fused(nc, local_sem=M.loc)
    g.remote_dma_fused(ns, local_sem=M.loc)
    g.wait_ge(M.loc, sent + landed)

    n = 1 + len(steps)
    for i in range(QT // 2):
        if i < len(steps):
            g.vector.wait_ge(M.vp, n + i)
            g.vector.tensor_tensor(T.AC[0:32, J * (i + 1):J * (i + 2)], T.AC[0:32, J * i:J * (i + 1)], T.TM[0:32, J * i:J * i + J],
                                   AluOpType.add).then_inc(M.vp, 1)
        a, b = 2 * i, 2 * i + 2
        g.vector.wait_ge(M["q%d" % [k for k, pc in enumerate(PIECES) if pc[0] <= a < pc[1]][0]], 16)
        g.vector.quantize_mx(T.WC[:, 128 * a:128 * b], T.WS[:, 128 * a:128 * b], T.WQ[:, 512 * a:512 * b]).then_inc(M.wq, 1)
    assert len(steps) <= QT // 2
    g.vector.wait_ge(M.vp, n + len(steps))
    a = J * len(steps)
    g.vector.tensor_scalar(T.AC[0:32, a + J:a + 2 * J], T.AC[0:32, a:a + J], KP, None, AluOpType.add).then_inc(M.vp, 1)
    g.vector.wait_ge(M.vp, n + len(steps) + 1)
    for p in range(0, 128, 32):
        g.vector.tensor_copy(T.V[p:p + 32, 0:2 * J], T.AC[0:32, a:a + 2 * J]).then_inc(M.pv, 1)

    e0 = len(near) * CAPP
    l0 = NE - 128
    hw = (1 + len(near)) * CAPP
    fw = len(far) * CAPP

    def product(o, c0, sem):
        g.tensor.matmul_mx(T.P[:, 512 * o:512 * o + 128], T.WC[:, 128 * o:128 * o + 128], T.WS[:, 128 * o:128 * o + 128],
                           T.EC[:, c0:c0 + 128], T.ES[:, c0:c0 + 128], True, True).then_inc(sem, 1)
    g.tensor.wait_ge(M.ex, 1)
    g.tensor.wait_ge(M.near, landed)
    for k in range(QT // 2):
        g.tensor.wait_ge(M.wq, k + 1)
        for o in (2 * k, 2 * k + 1):
            product(o, e0, M.em)
            src, dst = T.P[:, 512 * o + 128 - hw:512 * o + 128], T.S[:, KP * o:KP * o + hw]
            if o in BYV:
                g.vector.wait_ge(M.em, o + 1)
                g.vector.tensor_copy(dst, src).then_inc(M.ev, 1)
            else:
                g.scalar.wait_ge(M.em, o + 1)
                g.scalar.activation(dst, src, COPY).then_inc(M.ec, 1)
    g.tensor.wait_ge(M.far, far_increments(T, topo, core))
    for o in range(QT):
        g.tensor.wait_ge(M.ev if o in BYV else M.ec, len([k for k in range(o + 1) if (k in BYV) == (o in BYV)]))
        product(o, l0, M.lm)

    g.vector.wait_ge(M.pv, 4)
    g.scalar.wait_ge(M.pv, 4)

    def copy(o, e):
        src, dst = T.P[:, 512 * o + 128 - fw:512 * o + 128], T.S[:, KP * o + hw:KP * o + KP]
        e.wait_ge(M.lm, o + 1)
        if e is g.scalar:
            e.activation(dst, src, COPY).then_inc(M.sc, 1)
        else:
            e.tensor_copy(dst, src).then_inc(M.vc, 1)

    def pick(o, k, e, sem, n):
        win = T.S[:, KP * o:KP * (o + k)].indirect(T.V[:, 0:k * J])
        yo = T.YS[:, CW * o:CW * (o + k)]
        for s, v in ((M.vc, sem), (M.sc, n)):
            if v:
                e.wait_ge(s, v)
        if e is g.scalar:
            e.activation(yo, win, COPY).then_inc(M.so, 1)
        else:
            e.tensor_copy(yo, win).then_inc(M.vo, 1)
    for o in (0, 2):
        copy(o, g.vector)
    for o in (1, 3, 4, 5, 6, 7):
        copy(o, g.scalar)
    pick(0, 1, g.vector, 1, 0)
    pick(1, 2, g.vector, 2, 1)
    pick(3, 1, g.scalar, 0, 2)
    pick(4, 2, g.vector, 2, 4)
    pick(6, 2, g.scalar, 0, 6)
    for a, b, nv, ns in [(0, 1, 1, 0), (1, 4, 2, 1), (4, 8, 3, 2)]:
        g.sync.wait_ge(M.vo, nv)
        if ns:
            g.sync.wait_ge(M.so, ns)
        g.sync.dma_start(T.y[:, CW * a:CW * b], T.YS[:, CW * a:CW * b]).then_inc(M.st, 16)
    g.sync.wait_ge(M.st, 48)
